import numpy as np
import ml_dtypes


def mxq(x, axis, fmt="e4m3"):
    dtype, down = {"e4m3": (ml_dtypes.float8_e4m3fn, 7), "e5m2": (ml_dtypes.float8_e5m2, 14)}[fmt]
    v = np.moveaxis(np.asarray(x, np.float32).astype(ml_dtypes.bfloat16).astype(np.float64), axis, -1)
    blocks = v.reshape(v.shape[:-1] + (-1, 32))
    amax = np.abs(blocks).max(-1, keepdims=True)
    byte = np.maximum(np.where(amax > 0, np.frexp(amax)[1] - 1 + 127, 0) - down, 1)
    scale = np.exp2(byte - 127.0)
    codes = (blocks / scale).astype(np.float32).astype(dtype).astype(np.float64)
    return np.moveaxis((codes * scale).reshape(v.shape), -1, axis)


WIDE = False


def mx_kscale(k):
    if not WIDE:
        return np.ones(k)
    levels = np.array([10, -10, 5, -5, 0])
    if k % 512:
        return np.exp2(np.random.permutation(np.resize(levels, k // 32))).repeat(32)
    a = np.empty((k // 512, 16))
    for p in range(k // 512):
        a[p, :8] = np.random.permutation(np.resize(levels, 8))
        for g in range(8):
            far = levels[np.abs(levels - a[p, g]) >= 10]
            a[p, g + 8] = far[np.random.randint(len(far))]
    return np.exp2(a.ravel()).repeat(32)


def f64(x):
    return np.asarray(x).astype(np.float64)


def striped(idx):
    return np.tile(np.asarray(idx).reshape(-1, 16).T, (8, 1)).astype(np.uint16)


def unstriped(offs):
    return offs[:16].T.reshape(-1).astype(np.int64)


E2M1 = np.array([0.0, 0.5, 1.0, 1.5, 2.0, 3.0, 4.0, 6.0, -0.0, -0.5, -1.0, -1.5, -2.0, -3.0, -4.0, -6.0])


def pack_weight(w, fmt):
    k, n = w.shape
    w = f64(np.asarray(w, np.float32).astype(ml_dtypes.bfloat16)).reshape(k // 32, 32, n)
    amax = np.abs(w).max(1)
    if fmt == "e4m3":
        byte = np.frexp(amax)[1] - 1 + 127 - 7
    else:
        mant, ex = np.frexp(amax / 6.0)
        byte = np.where(mant > 0.5, ex, ex - 1) + 127
    byte = np.clip(np.where(amax > 0, byte, 1), 1, 254)
    scaled = (w * np.exp2(127.0 - byte)[:, None, :]).reshape(k, n).astype(np.float32)
    by_word = np.ascontiguousarray(scaled.reshape(k // 512, 128, 4, n).transpose(0, 1, 3, 2))
    if fmt == "e4m3":
        words = by_word.astype(ml_dtypes.float8_e4m3fn).view(np.uint8)
    else:
        c = by_word.astype(ml_dtypes.float4_e2m1fn).view(np.uint8) & 0xF
        words = (c[..., 0::2] | (c[..., 1::2] << 4)).reshape(k // 512, 128, 2 * n)
    return np.ascontiguousarray(words), np.ascontiguousarray(byte.astype(np.uint8).reshape(k // 512, 16, n))


def unpack_weight(words, scales, fmt):
    g, _, n = scales.shape
    words = np.ascontiguousarray(words).reshape(g, 128, n, -1)
    if fmt == "e4m3":
        vals = words.view(ml_dtypes.float8_e4m3fn).astype(np.float64)
    else:
        nib = np.empty((g, 128, n, 4), np.uint8)
        nib[..., 0::2] = words & 0xF
        nib[..., 1::2] = words >> 4
        vals = E2M1[nib]
    vals = vals * np.repeat(np.exp2(scales.astype(np.float64) - 127.0), 8, axis=1)[..., None]
    return vals.transpose(0, 1, 3, 2).reshape(g * 512, n)


def softplus(v):
    return np.log(1.0 + np.exp(v))


K, T, J, N = 1024, 2048, 512, 512


def setup_inputs():
    n = np.random.standard_normal
    idx = np.random.permutation(T)[:J]
    fk = mx_kscale(K)
    xqp = pack_weight(n((K, T)) / fk[:, None], "e4m3")
    wbp = pack_weight(n((K, N)) * 1 / np.sqrt(K) * fk[:, None], "e2m1")
    return {
        "xq_words": xqp[0],
        "xq_scales": xqp[1],
        "wa": (n((K, N)) * 1 / np.sqrt(K) * fk[:, None]).astype(np.float32),
        "wb_words": wbp[0],
        "wb_scales": wbp[1],
        "pg": (1.0 * n((N, T))).astype(np.float32),
        "offs": striped(idx),
    }


def reference(xq_words, xq_scales, wa, wb_words, wb_scales, pg, offs):
    idx = unstriped(offs)
    xqu = unpack_weight(xq_words, xq_scales, "e4m3")
    wbu = unpack_weight(wb_words, wb_scales, "e2m1")
    waq = mxq(f64(wa), 0, "e4m3")
    xqidxg = xqu[:, idx]
    p = waq.T @ xqidxg
    q = wbu.T @ xqidxg
    sp = softplus(p)
    sq_ = softplus(q)
    y = f64(pg)[:, idx] * sp / (sp + sq_ + 0.1)
    return y

@@ -1,0 +1,209 @@
+import math
+from contextlib import ExitStack
+
+import concourse.mybir as mybir
+from concourse.masks import make_identity
+
+K, T, J, N = 1024, 2048, 512, 512
+FLOPS = 2 * 2 * K * J * N
+
+F32 = mybir.dt.float32
+BF16 = mybir.dt.bfloat16
+I32 = mybir.dt.int32
+U32 = mybir.dt.uint32
+U16 = mybir.dt.uint16
+U8 = mybir.dt.uint8
+FP8X4 = mybir.dt.float8_e4m3fn_x4
+FP4X4 = mybir.dt.float4_e2m1fn_x4
+ALU = mybir.AluOpType
+ACT = mybir.ActivationFunctionType
+
+P = 128
+PACK = 4
+PASSES = K // (P * PACK)
+BLOCKS = N // P
+QUADS = 4
+LN_FLOOR = 2.0 ** -58
+KNEE = 20.0
+
+
+def tile_list_expert_share_of_sum_kernel(tc, xq_words, xq_scales, wa, wb_words, wb_scales, pg, offs, out):
+    nc = tc.nc
+    with ExitStack() as ctx:
+        keep = ctx.enter_context(tc.tile_pool(name="keep", bufs=1))
+        psum = ctx.enter_context(tc.psum_pool(name="psum", bufs=1))
+
+        def sb(shape, dtype, name):
+            return keep.tile(shape, dtype, name=name, align_bytes=64)
+
+        def cols(i):
+            return slice(i * P, (i + 1) * P)
+
+        offsets = keep.tile([P, J // 16], U16, name="offsets")
+        x_words = [sb([P, T], I32, "x_words%d" % z) for z in range(PASSES)]
+        x_scales = sb([P, PASSES, T], U8, "x_scales")
+        b_words = sb([P, PASSES, 2 * N], U8, "b_words")
+        b_scales = sb([P, PASSES, N], U8, "b_scales")
+        a_raw0 = sb([P, PACK, N], F32, "a_raw0")
+        a_raw1 = [sb([P, PACK, N // 2], F32, "a_raw1_%d" % h) for h in range(2)]
+        page = [sb([P, T], F32, "page%d" % i) for i in range(BLOCKS)]
+
+        nc.vector.memset(x_scales[:].rearrange("p z c -> p (z c)").bitcast(I32), 0)
+        nc.vector.memset(b_scales[:].rearrange("p z c -> p (z c)").bitcast(I32), 0)
+        warm_in = sb([P, 1], F32, "warm_in")
+        warm_out = sb([P, 1], F32, "warm_out")
+        nc.vector.memset(warm_in[:], 0.0)
+        nc.scalar.activation(warm_out[:], warm_in[:], ACT.Sigmoid)
+        ident = sb([P, P], F32, "ident")
+        make_identity(nc, ident[:])
+
+        def load_scales(tile, src):
+            for q in range(QUADS):
+                nc.sync.dma_start(
+                    out=tile[32 * q : 32 * q + 4, :, :].bitcast(I32),
+                    in_=src[:, 4 * q : 4 * q + 4, :].bitcast(I32).rearrange("z r c -> r z c"),
+                )
+
+        def load_words(z):
+            nc.sync.dma_start(out=x_words[z][:], in_=xq_words[z].rearrange("p c r -> p (c r)").bitcast(I32))
+
+        nc.sync.dma_start(offsets[:], offs)
+        load_words(0)
+        load_scales(x_scales, xq_scales)
+        nc.sync.dma_start(out=b_words[:].bitcast(I32), in_=wb_words.bitcast(I32).rearrange("z p c -> p z c"))
+        load_words(1)
+        load_scales(b_scales, wb_scales)
+        wa_rows = wa.rearrange("(z p t) n -> z p t n", z=PASSES, t=PACK)
+        nc.sync.dma_start(out=a_raw0[:], in_=wa_rows[0])
+        for h in range(2):
+            nc.sync.dma_start(out=a_raw1[h][:], in_=wa_rows[1][:, :, h * (N // 2) : (h + 1) * (N // 2)])
+        for i in range(BLOCKS):
+            nc.sync.dma_start(out=page[i][:], in_=pg[cols(i), :])
+
+        g_words = [sb([P, J], U32, "g_words%d" % z) for z in range(PASSES)]
+        g_scales = [sb([P, J], U8, "g_scales%d" % z) for z in range(PASSES)]
+        for z in range(PASSES):
+            nc.vector.tensor_copy(g_scales[z][:], x_scales[:, z, :].indirect(offsets[:]))
+            nc.vector.tensor_copy(g_words[z][:], x_words[z][:].bitcast(U32).indirect(offsets[:]))
+
+        q_bank = [psum.tile([P, N], F32, name="q_bank%d" % i) for i in range(BLOCKS)]
+        p_bank = [psum.tile([P, N], F32, name="p_bank%d" % i) for i in range(BLOCKS)]
+
+        for z, jb in [(0, 0), (0, 1), (1, 0), (1, 1), (0, 2), (1, 2), (0, 3), (1, 3)]:
+            if True:
+                nc.tensor.matmul_mx(
+                    q_bank[jb][:],
+                    lhsT=g_words[z][:, cols(jb)].bitcast(FP8X4),
+                    lhsT_scale=g_scales[z][:, cols(jb)],
+                    rhs=b_words[:, z, :].bitcast(FP4X4),
+                    rhs_scale=b_scales[:, z, :],
+                    start=(z == 0),
+                    stop=(z == PASSES - 1),
+                )
+
+        q_sig = sb([P, BLOCKS, N], F32, "q_sig")
+        for jb in range(BLOCKS):
+            nc.scalar.activation(q_sig[:, jb, :], q_bank[jb][:], ACT.Sigmoid, scale=-1.0)
+
+        def interleave(name, raw):
+            width = raw.shape[2]
+            grouped = sb([P, width, PACK], BF16, name)
+            nc.vector.tensor_copy(
+                out=grouped[:].rearrange("p (c i) t -> p c t i", i=4),
+                in_=raw.rearrange("p t (c i) -> p c t i", i=4),
+            )
+            return grouped
+
+        def quantize(name, grouped):
+            width = grouped.shape[1]
+            codes = sb([P, width], U32, name + "_codes")
+            scales = sb([P, width], U8, name + "_scales")
+            nc.vector.quantize_mx(codes[:].bitcast(FP8X4), scales[:], grouped[:].rearrange("p w t -> p (w t)"))
+            return codes, scales
+
+        def p_pass(z, i, codes, scales):
+            for jb in range(BLOCKS):
+                nc.tensor.matmul_mx(
+                    p_bank[i][:, cols(jb)],
+                    lhsT=g_words[z][:, cols(jb)].bitcast(FP8X4),
+                    lhsT_scale=g_scales[z][:, cols(jb)],
+                    rhs=codes.bitcast(FP8X4),
+                    rhs_scale=scales,
+                    start=(z == 0 and jb == 0),
+                    stop=(z == PASSES - 1 and jb == BLOCKS - 1),
+                )
+
+        halves = [interleave("a_bf0_%d" % h, a_raw0[:, :, h * (N // 2) : (h + 1) * (N // 2)]) for h in range(2)]
+        for h in range(2):
+            codes, scales = quantize("a_q0_%d" % h, halves[h])
+            for s in range(2):
+                p_pass(0, 2 * h + s, codes[:, cols(s)], scales[:, cols(s)])
+
+        p_sig = [sb([P, J], F32, "p_sig%d" % i) for i in range(BLOCKS)]
+        for h in range(2):
+            pair = [interleave("a_bf1_%d" % (2 * h + s), a_raw1[h][:, :, cols(s)]) for s in range(2)]
+            for s in range(2):
+                i = 2 * h + s
+                codes, scales = quantize("a_q1_%d" % i, pair[s])
+                p_pass(1, i, codes[:], scales[:])
+                nc.scalar.activation(p_sig[i][:], p_bank[i][:], ACT.Sigmoid, scale=-1.0)
+
+        q_relu = sb([P, BLOCKS, N], F32, "q_relu")
+        for jb in range(BLOCKS):
+            nc.vector.tensor_scalar(q_relu[:, jb, :], q_bank[jb][:], KNEE, -1.0, op0=ALU.max, op1=ALU.mult)
+
+        def turn(bank, src, start, stop):
+            for jb in range(BLOCKS):
+                nc.tensor.matmul(
+                    bank[:, cols(jb)], lhsT=src[:, jb, :], rhs=ident[:], is_transpose=True,
+                    start=(start and jb == 0), stop=(stop and jb == BLOCKS - 1),
+                )
+
+        sum_bank = q_bank
+        for i in range(BLOCKS):
+            turn(sum_bank[i], q_relu[:, :, cols(i)], True, False)
+
+        picked = [sb([P, J], F32, "picked%d" % i) for i in range(BLOCKS)]
+        nc.vector.tensor_copy(picked[0][:], page[0][:].indirect(offsets[:]))
+
+        floor = sb([P, 1], F32, "floor")
+        nc.scalar.activation(floor[:], p_sig[BLOCKS - 1][:, 0:1], ACT.Copy, bias=LN_FLOOR, scale=0.0)
+
+        q_cut = [sb([P, BLOCKS, P], F32, "q_cut%d" % i) for i in range(BLOCKS)]
+        for i in range(BLOCKS):
+            nc.gpsimd.tensor_scalar(q_cut[i][:], q_sig[:, :, cols(i)], math.exp(-KNEE), floor[:], op0=ALU.max, op1=ALU.add)
+
+        p_ln = [sb([P, J], F32, "p_ln%d" % i) for i in range(BLOCKS)]
+        p_soft = [sb([P, BLOCKS, P], F32, "p_soft%d" % i) for i in range(BLOCKS)]
+        for i in range(BLOCKS):
+            nc.scalar.activation(p_ln[i][:], p_sig[i][:], ACT.Ln, bias=floor[:])
+            nc.vector.scalar_tensor_tensor(
+                p_soft[i][:].rearrange("p b c -> p (b c)"), p_bank[i][:], -1.0, p_ln[i][:], op0=ALU.mult, op1=ALU.min
+            )
+            turn(sum_bank[i], p_soft[i], False, False)
+
+        q_ln = [sb([P, BLOCKS, P], F32, "q_ln%d" % i) for i in range(BLOCKS)]
+        for i in range(BLOCKS):
+            nc.scalar.activation(q_ln[i][:], q_cut[i][:], ACT.Ln, scale=math.exp(-0.1))
+            turn(sum_bank[i], q_ln[i], False, True)
+
+        sum_ln = [sb([P, J], F32, "sum_ln%d" % i) for i in range(BLOCKS)]
+        for i in range(BLOCKS):
+            nc.scalar.activation(sum_ln[i][:], sum_bank[i][:], ACT.Ln, bias=-KNEE, scale=-1.0)
+
+        for i in range(1, BLOCKS):
+            nc.vector.tensor_copy(picked[i][:], page[i][:].indirect(offsets[:]))
+
+        top = [sb([P, J], F32, "top%d" % i) for i in range(BLOCKS)]
+        for i in range(BLOCKS):
+            turn(p_bank[i], p_soft[i], True, True)
+            nc.vector.scalar_tensor_tensor(top[i][:], p_bank[i][:], -1.0, picked[i][:], op0=ALU.mult, op1=ALU.mult)
+
+        zero = sb([P, 1], F32, "zero")
+        nc.scalar.activation(zero[:], sum_ln[BLOCKS - 1][:, 0:1], ACT.Copy, bias=0.0, scale=0.0)
+        for i in range(BLOCKS):
+            inv = sb([P, J], F32, "inv%d" % i)
+            nc.scalar.activation(inv[:], sum_ln[i][:], ACT.Exp, bias=zero[:], scale=-1.0)
+            res = sb([P, J], F32, "res%d" % i)
+            nc.vector.tensor_tensor(res[:], top[i][:], inv[:], ALU.mult)
+            nc.sync.dma_start(out=out[cols(i), :], in_=res[:])

@@ -25,6 +25,8 @@ BLOCKS = N // P
 QUADS = 4
 LN_FLOOR = 2.0 ** -58
 KNEE = 20.0
+EARLY = 2
+LATE = BLOCKS - EARLY
 
 
 def tile_list_expert_share_of_sum_kernel(tc, xq_words, xq_scales, wa, wb_words, wb_scales, pg, offs, out):
@@ -33,8 +35,8 @@ def tile_list_expert_share_of_sum_kernel(tc, xq_words, xq_scales, wa, wb_words, 
         keep = ctx.enter_context(tc.tile_pool(name="keep", bufs=1))
         psum = ctx.enter_context(tc.psum_pool(name="psum", bufs=1))
 
-        def sb(shape, dtype, name):
-            return keep.tile(shape, dtype, name=name, align_bytes=64)
+        def sb(shape, dtype, name, tag=None):
+            return keep.tile(shape, dtype, name=name, tag=tag or name, align_bytes=64)
 
         def cols(i):
             return slice(i * P, (i + 1) * P)
@@ -44,8 +46,7 @@ def tile_list_expert_share_of_sum_kernel(tc, xq_words, xq_scales, wa, wb_words, 
         x_scales = sb([P, PASSES, T], U8, "x_scales")
         b_words = sb([P, PASSES, 2 * N], U8, "b_words")
         b_scales = sb([P, PASSES, N], U8, "b_scales")
-        a_raw0 = sb([P, PACK, N], F32, "a_raw0")
-        a_raw1 = [sb([P, PACK, N // 2], F32, "a_raw1_%d" % h) for h in range(2)]
+        a_raw = [[sb([P, PACK, N // 2], F32, "a_raw%d_%d" % (z, h)) for h in range(2)] for z in range(PASSES)]
         page = [sb([P, T], F32, "page%d" % i) for i in range(BLOCKS)]
 
         nc.vector.memset(x_scales[:].rearrange("p z c -> p (z c)").bitcast(I32), 0)
@@ -74,43 +75,40 @@ def tile_list_expert_share_of_sum_kernel(tc, xq_words, xq_scales, wa, wb_words, 
         load_words(1)
         load_scales(b_scales, wb_scales)
         wa_rows = wa.rearrange("(z p t) n -> z p t n", z=PASSES, t=PACK)
-        nc.sync.dma_start(out=a_raw0[:], in_=wa_rows[0])
         for h in range(2):
-            nc.sync.dma_start(out=a_raw1[h][:], in_=wa_rows[1][:, :, h * (N // 2) : (h + 1) * (N // 2)])
+            for z in range(PASSES):
+                nc.sync.dma_start(out=a_raw[z][h][:], in_=wa_rows[z][:, :, h * (N // 2) : (h + 1) * (N // 2)])
         for i in range(BLOCKS):
             nc.sync.dma_start(out=page[i][:], in_=pg[cols(i), :])
 
         g_words = [sb([P, J], U32, "g_words%d" % z) for z in range(PASSES)]
         g_scales = [sb([P, J], U8, "g_scales%d" % z) for z in range(PASSES)]
+        nc.vector.tensor_copy(g_words[0][:], x_words[0][:].bitcast(U32).indirect(offsets[:]))
         for z in range(PASSES):
             nc.vector.tensor_copy(g_scales[z][:], x_scales[:, z, :].indirect(offsets[:]))
-            nc.vector.tensor_copy(g_words[z][:], x_words[z][:].bitcast(U32).indirect(offsets[:]))
+        nc.vector.tensor_copy(g_words[1][:], x_words[1][:].bitcast(U32).indirect(offsets[:]))
 
         q_bank = [psum.tile([P, N], F32, name="q_bank%d" % i) for i in range(BLOCKS)]
         p_bank = [psum.tile([P, N], F32, name="p_bank%d" % i) for i in range(BLOCKS)]
 
-        for z, jb in [(0, 0), (0, 1), (1, 0), (1, 1), (0, 2), (1, 2), (0, 3), (1, 3)]:
-            if True:
+        def product(bank, z, codes, scales):
+            for jb in range(BLOCKS):
                 nc.tensor.matmul_mx(
-                    q_bank[jb][:],
+                    bank[:, cols(jb)],
                     lhsT=g_words[z][:, cols(jb)].bitcast(FP8X4),
                     lhsT_scale=g_scales[z][:, cols(jb)],
-                    rhs=b_words[:, z, :].bitcast(FP4X4),
-                    rhs_scale=b_scales[:, z, :],
-                    start=(z == 0),
-                    stop=(z == PASSES - 1),
+                    rhs=codes,
+                    rhs_scale=scales,
+                    start=(z == 0 and jb == 0),
+                    stop=(z == PASSES - 1 and jb == BLOCKS - 1),
                 )
 
-        q_sig = sb([P, BLOCKS, N], F32, "q_sig")
-        for jb in range(BLOCKS):
-            nc.scalar.activation(q_sig[:, jb, :], q_bank[jb][:], ACT.Sigmoid, scale=-1.0)
-
-        def interleave(name, raw):
+        def interleave(copy, name, raw):
             width = raw.shape[2]
             grouped = sb([P, width, PACK], BF16, name)
-            nc.vector.tensor_copy(
-                out=grouped[:].rearrange("p (c i) t -> p c t i", i=4),
-                in_=raw.rearrange("p t (c i) -> p c t i", i=4),
+            copy(
+                out=grouped[:],
+                in_=raw.rearrange("p t w -> p w t"),
             )
             return grouped
 
@@ -121,36 +119,30 @@ def tile_list_expert_share_of_sum_kernel(tc, xq_words, xq_scales, wa, wb_words, 
             nc.vector.quantize_mx(codes[:].bitcast(FP8X4), scales[:], grouped[:].rearrange("p w t -> p (w t)"))
             return codes, scales
 
-        def p_pass(z, i, codes, scales):
-            for jb in range(BLOCKS):
-                nc.tensor.matmul_mx(
-                    p_bank[i][:, cols(jb)],
-                    lhsT=g_words[z][:, cols(jb)].bitcast(FP8X4),
-                    lhsT_scale=g_scales[z][:, cols(jb)],
-                    rhs=codes.bitcast(FP8X4),
-                    rhs_scale=scales,
-                    start=(z == 0 and jb == 0),
-                    stop=(z == PASSES - 1 and jb == BLOCKS - 1),
-                )
+        on_scalar = [(0, 0), (0, 1)]
+        rounded = {(z, i): interleave(nc.scalar.copy, "a_bf%d_%d" % (z, i), a_raw[z][0][:, :, cols(i)]) for z, i in on_scalar}
 
-        halves = [interleave("a_bf0_%d" % h, a_raw0[:, :, h * (N // 2) : (h + 1) * (N // 2)]) for h in range(2)]
+        q_sig = [sb([P, J], F32, "q_sig%d" % i, tag=("a_raw0_0" if i == 0 else None)) for i in range(BLOCKS)]
         for h in range(2):
-            codes, scales = quantize("a_q0_%d" % h, halves[h])
-            for s in range(2):
-                p_pass(0, 2 * h + s, codes[:, cols(s)], scales[:, cols(s)])
+            for z in range(PASSES):
+                for i in (2 * h, 2 * h + 1):
+                    product(q_bank[i], z, b_words[:, z, 2 * P * i : 2 * P * (i + 1)].bitcast(FP4X4), b_scales[:, z, cols(i)])
+                    if z == PASSES - 1:
+                        nc.scalar.activation(q_sig[i][:], q_bank[i][:], ACT.Sigmoid, scale=-1.0)
 
         p_sig = [sb([P, J], F32, "p_sig%d" % i) for i in range(BLOCKS)]
         for h in range(2):
-            pair = [interleave("a_bf1_%d" % (2 * h + s), a_raw1[h][:, :, cols(s)]) for s in range(2)]
-            for s in range(2):
-                i = 2 * h + s
-                codes, scales = quantize("a_q1_%d" % i, pair[s])
-                p_pass(1, i, codes[:], scales[:])
-                nc.scalar.activation(p_sig[i][:], p_bank[i][:], ACT.Sigmoid, scale=-1.0)
-
-        q_relu = sb([P, BLOCKS, N], F32, "q_relu")
-        for jb in range(BLOCKS):
-            nc.vector.tensor_scalar(q_relu[:, jb, :], q_bank[jb][:], KNEE, -1.0, op0=ALU.max, op1=ALU.mult)
+            for z in range(PASSES):
+                for s in range(2):
+                    i = 2 * h + s
+                    if (z, i) not in rounded:
+                        rounded[(z, i)] = interleave(nc.vector.tensor_copy, "a_bf%d_%d" % (z, i), a_raw[z][h][:, :, cols(s)])
+                for s in range(2):
+                    i = 2 * h + s
+                    codes, scales = quantize("a_q%d_%d" % (z, i), rounded[(z, i)])
+                    product(p_bank[i], z, codes[:].bitcast(FP8X4), scales[:])
+                    if z == PASSES - 1:
+                        nc.scalar.activation(p_sig[i][:], p_bank[i][:], ACT.Sigmoid, scale=-1.0)
 
         def turn(bank, src, start, stop):
             for jb in range(BLOCKS):
@@ -159,45 +151,53 @@ def tile_list_expert_share_of_sum_kernel(tc, xq_words, xq_scales, wa, wb_words, 
                     start=(start and jb == 0), stop=(stop and jb == BLOCKS - 1),
                 )
 
-        sum_bank = q_bank
-        for i in range(BLOCKS):
-            turn(sum_bank[i], q_relu[:, :, cols(i)], True, False)
-
-        picked = [sb([P, J], F32, "picked%d" % i) for i in range(BLOCKS)]
-        nc.vector.tensor_copy(picked[0][:], page[0][:].indirect(offsets[:]))
-
         floor = sb([P, 1], F32, "floor")
         nc.scalar.activation(floor[:], p_sig[BLOCKS - 1][:, 0:1], ACT.Copy, bias=LN_FLOOR, scale=0.0)
 
-        q_cut = [sb([P, BLOCKS, P], F32, "q_cut%d" % i) for i in range(BLOCKS)]
-        for i in range(BLOCKS):
-            nc.gpsimd.tensor_scalar(q_cut[i][:], q_sig[:, :, cols(i)], math.exp(-KNEE), floor[:], op0=ALU.max, op1=ALU.add)
-
-        p_ln = [sb([P, J], F32, "p_ln%d" % i) for i in range(BLOCKS)]
-        p_soft = [sb([P, BLOCKS, P], F32, "p_soft%d" % i) for i in range(BLOCKS)]
-        for i in range(BLOCKS):
-            nc.scalar.activation(p_ln[i][:], p_sig[i][:], ACT.Ln, bias=floor[:])
+        def minus_softplus(name, sig, bank):
+            ln = sb([P, J], F32, name + "_ln")
+            soft = sb([P, BLOCKS, P], F32, name + "_soft")
+            nc.scalar.activation(ln[:], sig[:], ACT.Ln, bias=floor[:])
             nc.vector.scalar_tensor_tensor(
-                p_soft[i][:].rearrange("p b c -> p (b c)"), p_bank[i][:], -1.0, p_ln[i][:], op0=ALU.mult, op1=ALU.min
+                soft[:].rearrange("p b c -> p (b c)"), bank[:], -1.0, ln[:], op0=ALU.mult, op1=ALU.min
             )
-            turn(sum_bank[i], p_soft[i], False, False)
+            return soft
 
-        q_ln = [sb([P, BLOCKS, P], F32, "q_ln%d" % i) for i in range(BLOCKS)]
+        early = sb([P, 2 * EARLY * J], F32, "early", tag="a_raw1_1")
+        sum_bank = [p_bank[i] if i < LATE else q_bank[i] for i in range(BLOCKS)]
+        q_cut = [early[:, (EARLY + i) * J : (EARLY + i + 1) * J] for i in range(EARLY)]
+        for i in range(EARLY):
+            over = early[:, i * J : (i + 1) * J]
+            nc.vector.tensor_scalar(over, q_bank[LATE + i][:], KNEE, -1.0, op0=ALU.max, op1=ALU.mult)
+            turn(sum_bank[LATE + i], over.rearrange("p (b c) -> p b c", b=BLOCKS), True, False)
+            nc.vector.tensor_scalar_max(q_cut[i], q_sig[LATE + i][:], math.exp(-KNEE))
+
+        p_soft = []
         for i in range(BLOCKS):
-            nc.scalar.activation(q_ln[i][:], q_cut[i][:], ACT.Ln, scale=math.exp(-0.1))
-            turn(sum_bank[i], q_ln[i], False, True)
+            p_soft.append(minus_softplus("p%d" % i, p_sig[i], p_bank[i]))
+            turn(sum_bank[i], p_soft[i], i < LATE, False)
+            if i >= LATE:
+                q_soft = sb([P, BLOCKS, P], F32, "q%d_soft" % i)
+                nc.scalar.activation(
+                    q_soft[:].rearrange("p b c -> p (b c)"), q_cut[i - LATE], ACT.Ln, bias=floor[:], scale=math.exp(-0.1)
+                )
+            else:
+                q_soft = minus_softplus("q%d" % i, q_sig[i], q_bank[i])
+            turn(sum_bank[i], q_soft, False, True)
 
         sum_ln = [sb([P, J], F32, "sum_ln%d" % i) for i in range(BLOCKS)]
         for i in range(BLOCKS):
-            nc.scalar.activation(sum_ln[i][:], sum_bank[i][:], ACT.Ln, bias=-KNEE, scale=-1.0)
+            nc.scalar.activation(sum_ln[i][:], sum_bank[i][:], ACT.Ln, bias=(0.1 if i < LATE else -KNEE), scale=-1.0)
 
-        for i in range(1, BLOCKS):
-            nc.vector.tensor_copy(picked[i][:], page[i][:].indirect(offsets[:]))
+        late = sb([P, 2 * J], F32, "picked_late", tag="p%d_ln" % (BLOCKS - 1))
+        picked = [sb([P, J], F32, "picked%d" % i)[:] for i in range(2)] + [late[:, 0:J], late[:, J : 2 * J]]
+        for i in range(BLOCKS):
+            nc.vector.tensor_copy(picked[i], page[i][:].indirect(offsets[:]))
 
         top = [sb([P, J], F32, "top%d" % i) for i in range(BLOCKS)]
         for i in range(BLOCKS):
-            turn(p_bank[i], p_soft[i], True, True)
-            nc.vector.scalar_tensor_tensor(top[i][:], p_bank[i][:], -1.0, picked[i][:], op0=ALU.mult, op1=ALU.mult)
+            turn(sum_bank[i], p_soft[i], True, True)
+            nc.vector.scalar_tensor_tensor(top[i][:], sum_bank[i][:], -1.0, picked[i], op0=ALU.mult, op1=ALU.mult)
 
         zero = sb([P, 1], F32, "zero")
         nc.scalar.activation(zero[:], sum_ln[BLOCKS - 1][:, 0:1], ACT.Copy, bias=0.0, scale=0.0)

@@ -23,10 +23,12 @@ PACK = 4
 PASSES = K // (P * PACK)
 BLOCKS = N // P
 QUADS = 4
-LN_FLOOR = 2.0 ** -58
+HALVES = 2
+PER_HALF = BLOCKS // HALVES
+OFFSET = 0.1
 KNEE = 20.0
-EARLY = 2
-LATE = BLOCKS - EARLY
+BEFORE = 2
+AFTER = BLOCKS - BEFORE
 
 
 def tile_list_expert_share_of_sum_kernel(tc, xq_words, xq_scales, wa, wb_words, wb_scales, pg, offs, out):
@@ -41,20 +43,28 @@ def tile_list_expert_share_of_sum_kernel(tc, xq_words, xq_scales, wa, wb_words, 
         def cols(i):
             return slice(i * P, (i + 1) * P)
 
+        def part(tile, i):
+            return tile[:, i * J : (i + 1) * J]
+
         offsets = keep.tile([P, J // 16], U16, name="offsets")
         x_words = [sb([P, T], I32, "x_words%d" % z) for z in range(PASSES)]
         x_scales = sb([P, PASSES, T], U8, "x_scales")
         b_words = sb([P, PASSES, 2 * N], U8, "b_words")
         b_scales = sb([P, PASSES, N], U8, "b_scales")
-        a_raw = [[sb([P, PACK, N // 2], F32, "a_raw%d_%d" % (z, h)) for h in range(2)] for z in range(PASSES)]
+        a_raw = [[sb([P, PACK, N // HALVES], F32, "a_raw%d_%d" % (z, h)) for h in range(HALVES)] for z in range(PASSES)]
         page = [sb([P, T], F32, "page%d" % i) for i in range(BLOCKS)]
 
         nc.vector.memset(x_scales[:].rearrange("p z c -> p (z c)").bitcast(I32), 0)
         nc.vector.memset(b_scales[:].rearrange("p z c -> p (z c)").bitcast(I32), 0)
-        warm_in = sb([P, 1], F32, "warm_in")
-        warm_out = sb([P, 1], F32, "warm_out")
-        nc.vector.memset(warm_in[:], 0.0)
-        nc.scalar.activation(warm_out[:], warm_in[:], ACT.Sigmoid)
+
+        sig_bias = sb([P, 1], F32, "sig_bias", tag="ln_after")
+        sig_scale = sb([P, 1], F32, "sig_scale", tag="ln_before")
+        minus_knee = sb([P, 1], F32, "minus_knee", tag="inv")
+        nc.gpsimd.memset(minus_knee[:], -KNEE)
+        nc.gpsimd.memset(sig_bias[:], 0.0)
+        nc.gpsimd.memset(sig_scale[:], -1.0)
+        ln_floor = sb([P, 1], F32, "ln_floor")
+        nc.scalar.activation(ln_floor[:], minus_knee[:], ACT.Sigmoid, scale=2.0)
         ident = sb([P, P], F32, "ident")
         make_identity(nc, ident[:])
 
@@ -68,16 +78,16 @@ def tile_list_expert_share_of_sum_kernel(tc, xq_words, xq_scales, wa, wb_words, 
         def load_words(z):
             nc.sync.dma_start(out=x_words[z][:], in_=xq_words[z].rearrange("p c r -> p (c r)").bitcast(I32))
 
-        nc.sync.dma_start(offsets[:], offs)
         load_words(0)
+        nc.sync.dma_start(offsets[:], offs)
         load_scales(x_scales, xq_scales)
         nc.sync.dma_start(out=b_words[:].bitcast(I32), in_=wb_words.bitcast(I32).rearrange("z p c -> p z c"))
         load_words(1)
         load_scales(b_scales, wb_scales)
         wa_rows = wa.rearrange("(z p t) n -> z p t n", z=PASSES, t=PACK)
-        for h in range(2):
+        for h in range(HALVES):
             for z in range(PASSES):
-                nc.sync.dma_start(out=a_raw[z][h][:], in_=wa_rows[z][:, :, h * (N // 2) : (h + 1) * (N // 2)])
+                nc.sync.dma_start(out=a_raw[z][h][:], in_=wa_rows[z][:, :, h * (N // HALVES) : (h + 1) * (N // HALVES)])
         for i in range(BLOCKS):
             nc.sync.dma_start(out=page[i][:], in_=pg[cols(i), :])
 
@@ -103,94 +113,84 @@ def tile_list_expert_share_of_sum_kernel(tc, xq_words, xq_scales, wa, wb_words, 
                     stop=(z == PASSES - 1 and jb == BLOCKS - 1),
                 )
 
-        def interleave(copy, name, raw):
-            width = raw.shape[2]
-            grouped = sb([P, width, PACK], BF16, name)
-            copy(
-                out=grouped[:],
-                in_=raw.rearrange("p t w -> p w t"),
-            )
+        def interleave(copy, z, i):
+            grouped = sb([P, P, PACK], BF16, "a_bf%d_%d" % (z, i))
+            copy(out=grouped[:], in_=a_raw[z][i // PER_HALF][:, :, cols(i % PER_HALF)].rearrange("p t w -> p w t"))
             return grouped
 
         def quantize(name, grouped):
-            width = grouped.shape[1]
-            codes = sb([P, width], U32, name + "_codes")
-            scales = sb([P, width], U8, name + "_scales")
+            codes = sb([P, P], U32, name + "_codes")
+            scales = sb([P, P], U8, name + "_scales")
             nc.vector.quantize_mx(codes[:].bitcast(FP8X4), scales[:], grouped[:].rearrange("p w t -> p (w t)"))
             return codes, scales
 
-        on_scalar = [(0, 0), (0, 1)]
-        rounded = {(z, i): interleave(nc.scalar.copy, "a_bf%d_%d" % (z, i), a_raw[z][0][:, :, cols(i)]) for z, i in on_scalar}
+        rounded = {(0, i): interleave(nc.scalar.copy, 0, i) for i in range(PER_HALF)}
 
         q_sig = [sb([P, J], F32, "q_sig%d" % i, tag=("a_raw0_0" if i == 0 else None)) for i in range(BLOCKS)]
-        for h in range(2):
+        for h in range(HALVES):
             for z in range(PASSES):
-                for i in (2 * h, 2 * h + 1):
+                for i in range(h * PER_HALF, (h + 1) * PER_HALF):
                     product(q_bank[i], z, b_words[:, z, 2 * P * i : 2 * P * (i + 1)].bitcast(FP4X4), b_scales[:, z, cols(i)])
                     if z == PASSES - 1:
                         nc.scalar.activation(q_sig[i][:], q_bank[i][:], ACT.Sigmoid, scale=-1.0)
 
         p_sig = [sb([P, J], F32, "p_sig%d" % i) for i in range(BLOCKS)]
-        for h in range(2):
+        for h in range(HALVES):
             for z in range(PASSES):
-                for s in range(2):
-                    i = 2 * h + s
+                for i in range(h * PER_HALF, (h + 1) * PER_HALF):
                     if (z, i) not in rounded:
-                        rounded[(z, i)] = interleave(nc.vector.tensor_copy, "a_bf%d_%d" % (z, i), a_raw[z][h][:, :, cols(s)])
-                for s in range(2):
-                    i = 2 * h + s
+                        rounded[(z, i)] = interleave(nc.vector.tensor_copy, z, i)
+                for i in range(h * PER_HALF, (h + 1) * PER_HALF):
                     codes, scales = quantize("a_q%d_%d" % (z, i), rounded[(z, i)])
                     product(p_bank[i], z, codes[:].bitcast(FP8X4), scales[:])
                     if z == PASSES - 1:
-                        nc.scalar.activation(p_sig[i][:], p_bank[i][:], ACT.Sigmoid, scale=-1.0)
+                        nc.scalar.activation(p_sig[i][:], p_bank[i][:], ACT.Sigmoid, bias=sig_bias[:], scale=sig_scale[:])
 
         def turn(bank, src, start, stop):
             for jb in range(BLOCKS):
                 nc.tensor.matmul(
-                    bank[:, cols(jb)], lhsT=src[:, jb, :], rhs=ident[:], is_transpose=True,
+                    bank[:, cols(jb)], lhsT=src[:, cols(jb)], rhs=ident[:], is_transpose=True,
                     start=(start and jb == 0), stop=(stop and jb == BLOCKS - 1),
                 )
 
-        floor = sb([P, 1], F32, "floor")
-        nc.scalar.activation(floor[:], p_sig[BLOCKS - 1][:, 0:1], ACT.Copy, bias=LN_FLOOR, scale=0.0)
+        ln_after = sb([P, (BLOCKS + AFTER) * J], F32, "ln_after")
+        ln_before = sb([P, BEFORE * J], F32, "ln_before")
 
-        def minus_softplus(name, sig, bank):
-            ln = sb([P, J], F32, name + "_ln")
-            soft = sb([P, BLOCKS, P], F32, name + "_soft")
-            nc.scalar.activation(ln[:], sig[:], ACT.Ln, bias=floor[:])
-            nc.vector.scalar_tensor_tensor(
-                soft[:].rearrange("p b c -> p (b c)"), bank[:], -1.0, ln[:], op0=ALU.mult, op1=ALU.min
-            )
+        def minus_softplus(name, ln, sig, bank):
+            soft = sb([P, J], F32, name + "_soft")
+            nc.scalar.activation(ln, sig[:], ACT.Ln, bias=ln_floor[:])
+            nc.vector.scalar_tensor_tensor(soft[:], bank[:], -1.0, ln, op0=ALU.mult, op1=ALU.min)
             return soft
 
-        early = sb([P, 2 * EARLY * J], F32, "early", tag="a_raw1_1")
-        sum_bank = [p_bank[i] if i < LATE else q_bank[i] for i in range(BLOCKS)]
-        q_cut = [early[:, (EARLY + i) * J : (EARLY + i + 1) * J] for i in range(EARLY)]
-        for i in range(EARLY):
-            over = early[:, i * J : (i + 1) * J]
-            nc.vector.tensor_scalar(over, q_bank[LATE + i][:], KNEE, -1.0, op0=ALU.max, op1=ALU.mult)
-            turn(sum_bank[LATE + i], over.rearrange("p (b c) -> p b c", b=BLOCKS), True, False)
-            nc.vector.tensor_scalar_max(q_cut[i], q_sig[LATE + i][:], math.exp(-KNEE))
+        sum_bank = [p_bank[i] if i < AFTER else q_bank[i] for i in range(BLOCKS)]
+
+        guard = sb([P, 2 * BEFORE * J], F32, "guard", tag="a_raw1_1")
+        for e in range(BEFORE):
+            i = AFTER + e
+            nc.vector.tensor_scalar(part(guard, e), q_bank[i][:], KNEE, -1.0, op0=ALU.max, op1=ALU.mult)
+            turn(sum_bank[i], part(guard, e), True, False)
+            nc.vector.tensor_scalar_max(part(guard, BEFORE + e), q_sig[i][:], math.exp(-KNEE))
 
         p_soft = []
         for i in range(BLOCKS):
-            p_soft.append(minus_softplus("p%d" % i, p_sig[i], p_bank[i]))
-            turn(sum_bank[i], p_soft[i], i < LATE, False)
-            if i >= LATE:
-                q_soft = sb([P, BLOCKS, P], F32, "q%d_soft" % i)
-                nc.scalar.activation(
-                    q_soft[:].rearrange("p b c -> p (b c)"), q_cut[i - LATE], ACT.Ln, bias=floor[:], scale=math.exp(-0.1)
-                )
+            p_soft.append(minus_softplus("p%d" % i, part(ln_after, i), p_sig[i], p_bank[i]))
+            turn(sum_bank[i], p_soft[i], i < AFTER, False)
+            if i < AFTER:
+                q_soft = minus_softplus("q%d" % i, part(ln_after, BLOCKS + i), q_sig[i], q_bank[i])
             else:
-                q_soft = minus_softplus("q%d" % i, q_sig[i], q_bank[i])
+                q_soft = part(ln_before, i - AFTER)
+                nc.scalar.activation(q_soft, part(guard, BEFORE + i - AFTER), ACT.Ln, scale=math.exp(-OFFSET))
             turn(sum_bank[i], q_soft, False, True)
 
         sum_ln = [sb([P, J], F32, "sum_ln%d" % i) for i in range(BLOCKS)]
         for i in range(BLOCKS):
-            nc.scalar.activation(sum_ln[i][:], sum_bank[i][:], ACT.Ln, bias=(0.1 if i < LATE else -KNEE), scale=-1.0)
+            nc.scalar.activation(
+                sum_ln[i][:], sum_bank[i][:], ACT.Ln, bias=(OFFSET if i < AFTER else minus_knee[:]), scale=-1.0
+            )
 
-        late = sb([P, 2 * J], F32, "picked_late", tag="p%d_ln" % (BLOCKS - 1))
-        picked = [sb([P, J], F32, "picked%d" % i)[:] for i in range(2)] + [late[:, 0:J], late[:, J : 2 * J]]
+        picked_late = sb([P, (BLOCKS // 2) * J], F32, "picked_late", tag="ln_after")
+        picked = [sb([P, J], F32, "picked%d" % i)[:] for i in range(BLOCKS // 2)]
+        picked.extend([part(picked_late, e) for e in range(BLOCKS // 2)])
         for i in range(BLOCKS):
             nc.vector.tensor_copy(picked[i], page[i][:].indirect(offsets[:]))
 
@@ -199,11 +199,9 @@ def tile_list_expert_share_of_sum_kernel(tc, xq_words, xq_scales, wa, wb_words, 
             turn(sum_bank[i], p_soft[i], True, True)
             nc.vector.scalar_tensor_tensor(top[i][:], sum_bank[i][:], -1.0, picked[i], op0=ALU.mult, op1=ALU.mult)
 
-        zero = sb([P, 1], F32, "zero")
-        nc.scalar.activation(zero[:], sum_ln[BLOCKS - 1][:, 0:1], ACT.Copy, bias=0.0, scale=0.0)
+        inv = sb([P, BLOCKS * J], F32, "inv")
         for i in range(BLOCKS):
-            inv = sb([P, J], F32, "inv%d" % i)
-            nc.scalar.activation(inv[:], sum_ln[i][:], ACT.Exp, bias=zero[:], scale=-1.0)
+            nc.scalar.activation(part(inv, i), sum_ln[i][:], ACT.Exp, scale=-1.0)
             res = sb([P, J], F32, "res%d" % i)
-            nc.vector.tensor_tensor(res[:], top[i][:], inv[:], ALU.mult)
+            nc.vector.tensor_tensor(res[:], top[i][:], part(inv, i), ALU.mult)
             nc.sync.dma_start(out=out[cols(i), :], in_=res[:])

import math
from contextlib import ExitStack

import concourse.mybir as mybir
from concourse.masks import make_identity

K, T, J, N = 1024, 2048, 512, 512
FLOPS = 2 * 2 * K * J * N

F32 = mybir.dt.float32
BF16 = mybir.dt.bfloat16
I32 = mybir.dt.int32
U32 = mybir.dt.uint32
U16 = mybir.dt.uint16
U8 = mybir.dt.uint8
FP8X4 = mybir.dt.float8_e4m3fn_x4
FP4X4 = mybir.dt.float4_e2m1fn_x4
ALU = mybir.AluOpType
ACT = mybir.ActivationFunctionType

P = 128
PACK = 4
PASSES = K // (P * PACK)
BLOCKS = N // P
QUADS = 4
HALVES = 2
PER_HALF = BLOCKS // HALVES
OFFSET = 0.1
KNEE = 20.0
BEFORE = 2
AFTER = BLOCKS - BEFORE


def tile_list_expert_share_of_sum_kernel(tc, xq_words, xq_scales, wa, wb_words, wb_scales, pg, offs, out):
    nc = tc.nc
    with ExitStack() as ctx:
        keep = ctx.enter_context(tc.tile_pool(name="keep", bufs=1))
        psum = ctx.enter_context(tc.psum_pool(name="psum", bufs=1))

        def sb(shape, dtype, name, tag=None):
            return keep.tile(shape, dtype, name=name, tag=tag or name, align_bytes=64)

        def cols(i):
            return slice(i * P, (i + 1) * P)

        def part(tile, i):
            return tile[:, i * J : (i + 1) * J]

        offsets = keep.tile([P, J // 16], U16, name="offsets")
        x_words = [sb([P, T], I32, "x_words%d" % z) for z in range(PASSES)]
        x_scales = sb([P, PASSES, T], U8, "x_scales")
        b_words = sb([P, PASSES, 2 * N], U8, "b_words")
        b_scales = sb([P, PASSES, N], U8, "b_scales")
        a_raw = [[sb([P, PACK, N // HALVES], F32, "a_raw%d_%d" % (z, h)) for h in range(HALVES)] for z in range(PASSES)]
        page = [sb([P, T], F32, "page%d" % i) for i in range(BLOCKS)]

        nc.vector.memset(x_scales[:].rearrange("p z c -> p (z c)").bitcast(I32), 0)
        nc.vector.memset(b_scales[:].rearrange("p z c -> p (z c)").bitcast(I32), 0)

        sig_bias = sb([P, 1], F32, "sig_bias", tag="ln_after")
        sig_scale = sb([P, 1], F32, "sig_scale", tag="ln_before")
        minus_knee = sb([P, 1], F32, "minus_knee", tag="inv")
        nc.gpsimd.memset(minus_knee[:], -KNEE)
        nc.gpsimd.memset(sig_bias[:], 0.0)
        nc.gpsimd.memset(sig_scale[:], -1.0)
        ln_floor = sb([P, 1], F32, "ln_floor")
        nc.scalar.activation(ln_floor[:], minus_knee[:], ACT.Sigmoid, scale=2.0)
        ident = sb([P, P], F32, "ident")
        make_identity(nc, ident[:])

        def load_scales(tile, src):
            for q in range(QUADS):
                nc.sync.dma_start(
                    out=tile[32 * q : 32 * q + 4, :, :].bitcast(I32),
                    in_=src[:, 4 * q : 4 * q + 4, :].bitcast(I32).rearrange("z r c -> r z c"),
                )

        def load_words(z):
            nc.sync.dma_start(out=x_words[z][:], in_=xq_words[z].rearrange("p c r -> p (c r)").bitcast(I32))

        load_words(0)
        nc.sync.dma_start(offsets[:], offs)
        load_scales(x_scales, xq_scales)
        nc.sync.dma_start(out=b_words[:].bitcast(I32), in_=wb_words.bitcast(I32).rearrange("z p c -> p z c"))
        load_words(1)
        load_scales(b_scales, wb_scales)
        wa_rows = wa.rearrange("(z p t) n -> z p t n", z=PASSES, t=PACK)
        for h in range(HALVES):
            for z in range(PASSES):
                nc.sync.dma_start(out=a_raw[z][h][:], in_=wa_rows[z][:, :, h * (N // HALVES) : (h + 1) * (N // HALVES)])
        for i in range(BLOCKS):
            nc.sync.dma_start(out=page[i][:], in_=pg[cols(i), :])

        g_words = [sb([P, J], U32, "g_words%d" % z) for z in range(PASSES)]
        g_scales = [sb([P, J], U8, "g_scales%d" % z) for z in range(PASSES)]
        nc.vector.tensor_copy(g_words[0][:], x_words[0][:].bitcast(U32).indirect(offsets[:]))
        for z in range(PASSES):
            nc.vector.tensor_copy(g_scales[z][:], x_scales[:, z, :].indirect(offsets[:]))
        nc.vector.tensor_copy(g_words[1][:], x_words[1][:].bitcast(U32).indirect(offsets[:]))

        q_bank = [psum.tile([P, N], F32, name="q_bank%d" % i) for i in range(BLOCKS)]
        p_bank = [psum.tile([P, N], F32, name="p_bank%d" % i) for i in range(BLOCKS)]

        def product(bank, z, codes, scales):
            for jb in range(BLOCKS):
                nc.tensor.matmul_mx(
                    bank[:, cols(jb)],
                    lhsT=g_words[z][:, cols(jb)].bitcast(FP8X4),
                    lhsT_scale=g_scales[z][:, cols(jb)],
                    rhs=codes,
                    rhs_scale=scales,
                    start=(z == 0 and jb == 0),
                    stop=(z == PASSES - 1 and jb == BLOCKS - 1),
                )

        def interleave(copy, z, i):
            grouped = sb([P, P, PACK], BF16, "a_bf%d_%d" % (z, i))
            copy(out=grouped[:], in_=a_raw[z][i // PER_HALF][:, :, cols(i % PER_HALF)].rearrange("p t w -> p w t"))
            return grouped

        def quantize(name, grouped):
            codes = sb([P, P], U32, name + "_codes")
            scales = sb([P, P], U8, name + "_scales")
            nc.vector.quantize_mx(codes[:].bitcast(FP8X4), scales[:], grouped[:].rearrange("p w t -> p (w t)"))
            return codes, scales

        rounded = {(0, i): interleave(nc.scalar.copy, 0, i) for i in range(PER_HALF)}

        q_sig = [sb([P, J], F32, "q_sig%d" % i, tag=("a_raw0_0" if i == 0 else None)) for i in range(BLOCKS)]
        for h in range(HALVES):
            for z in range(PASSES):
                for i in range(h * PER_HALF, (h + 1) * PER_HALF):
                    product(q_bank[i], z, b_words[:, z, 2 * P * i : 2 * P * (i + 1)].bitcast(FP4X4), b_scales[:, z, cols(i)])
                    if z == PASSES - 1:
                        nc.scalar.activation(q_sig[i][:], q_bank[i][:], ACT.Sigmoid, scale=-1.0)

        p_sig = [sb([P, J], F32, "p_sig%d" % i) for i in range(BLOCKS)]
        for h in range(HALVES):
            for z in range(PASSES):
                for i in range(h * PER_HALF, (h + 1) * PER_HALF):
                    if (z, i) not in rounded:
                        rounded[(z, i)] = interleave(nc.vector.tensor_copy, z, i)
                for i in range(h * PER_HALF, (h + 1) * PER_HALF):
                    codes, scales = quantize("a_q%d_%d" % (z, i), rounded[(z, i)])
                    product(p_bank[i], z, codes[:].bitcast(FP8X4), scales[:])
                    if z == PASSES - 1:
                        nc.scalar.activation(p_sig[i][:], p_bank[i][:], ACT.Sigmoid, bias=sig_bias[:], scale=sig_scale[:])

        def turn(bank, src, start, stop):
            for jb in range(BLOCKS):
                nc.tensor.matmul(
                    bank[:, cols(jb)], lhsT=src[:, cols(jb)], rhs=ident[:], is_transpose=True,
                    start=(start and jb == 0), stop=(stop and jb == BLOCKS - 1),
                )

        ln_after = sb([P, (BLOCKS + AFTER) * J], F32, "ln_after")
        ln_before = sb([P, BEFORE * J], F32, "ln_before")

        def minus_softplus(name, ln, sig, bank):
            soft = sb([P, J], F32, name + "_soft")
            nc.scalar.activation(ln, sig[:], ACT.Ln, bias=ln_floor[:])
            nc.vector.scalar_tensor_tensor(soft[:], bank[:], -1.0, ln, op0=ALU.mult, op1=ALU.min)
            return soft

        sum_bank = [p_bank[i] if i < AFTER else q_bank[i] for i in range(BLOCKS)]

        guard = sb([P, 2 * BEFORE * J], F32, "guard", tag="a_raw1_1")
        for e in range(BEFORE):
            i = AFTER + e
            nc.vector.tensor_scalar(part(guard, e), q_bank[i][:], KNEE, -1.0, op0=ALU.max, op1=ALU.mult)
            turn(sum_bank[i], part(guard, e), True, False)
            nc.vector.tensor_scalar_max(part(guard, BEFORE + e), q_sig[i][:], math.exp(-KNEE))

        p_soft = []
        for i in range(BLOCKS):
            p_soft.append(minus_softplus("p%d" % i, part(ln_after, i), p_sig[i], p_bank[i]))
            turn(sum_bank[i], p_soft[i], i < AFTER, False)
            if i < AFTER:
                q_soft = minus_softplus("q%d" % i, part(ln_after, BLOCKS + i), q_sig[i], q_bank[i])
            else:
                q_soft = part(ln_before, i - AFTER)
                nc.scalar.activation(q_soft, part(guard, BEFORE + i - AFTER), ACT.Ln, scale=math.exp(-OFFSET))
            turn(sum_bank[i], q_soft, False, True)

        sum_ln = [sb([P, J], F32, "sum_ln%d" % i) for i in range(BLOCKS)]
        for i in range(BLOCKS):
            nc.scalar.activation(
                sum_ln[i][:], sum_bank[i][:], ACT.Ln, bias=(OFFSET if i < AFTER else minus_knee[:]), scale=-1.0
            )

        picked_late = sb([P, (BLOCKS // 2) * J], F32, "picked_late", tag="ln_after")
        picked = [sb([P, J], F32, "picked%d" % i)[:] for i in range(BLOCKS // 2)]
        picked.extend([part(picked_late, e) for e in range(BLOCKS // 2)])
        for i in range(BLOCKS):
            nc.vector.tensor_copy(picked[i], page[i][:].indirect(offsets[:]))

        top = [sb([P, J], F32, "top%d" % i) for i in range(BLOCKS)]
        for i in range(BLOCKS):
            turn(sum_bank[i], p_soft[i], True, True)
            nc.vector.scalar_tensor_tensor(top[i][:], sum_bank[i][:], -1.0, picked[i], op0=ALU.mult, op1=ALU.mult)

        inv = sb([P, BLOCKS * J], F32, "inv")
        for i in range(BLOCKS):
            nc.scalar.activation(part(inv, i), sum_ln[i][:], ACT.Exp, scale=-1.0)
            res = sb([P, J], F32, "res%d" % i)
            nc.vector.tensor_tensor(res[:], top[i][:], part(inv, i), ALU.mult)
            nc.sync.dma_start(out=out[cols(i), :], in_=res[:])
